import numpy as np
import ml_dtypes


def mxq(x, axis, fmt="e4m3"):
    dtype, down = {"e4m3": (ml_dtypes.float8_e4m3fn, 7), "e5m2": (ml_dtypes.float8_e5m2, 14)}[fmt]
    v = np.moveaxis(np.asarray(x, np.float32).astype(ml_dtypes.bfloat16).astype(np.float64), axis, -1)
    blocks = v.reshape(v.shape[:-1] + (-1, 32))
    amax = np.abs(blocks).max(-1, keepdims=True)
    byte = np.maximum(np.where(amax > 0, np.frexp(amax)[1] - 1 + 127, 0) - down, 1)
    scale = np.exp2(byte - 127.0)
    codes = (blocks / scale).astype(np.float32).astype(dtype).astype(np.float64)
    return np.moveaxis((codes * scale).reshape(v.shape), -1, axis)


WIDE = False


def mx_kscale(k):
    if not WIDE:
        return np.ones(k)
    levels = np.array([30, -30])
    if k % 512:
        return np.exp2(np.random.permutation(np.resize(levels, k // 32))).repeat(32)
    a = np.empty((k // 512, 16))
    for p in range(k // 512):
        a[p, :8] = np.random.permutation(np.resize(levels, 8))
        for g in range(8):
            far = levels[np.abs(levels - a[p, g]) >= 10]
            a[p, g + 8] = far[np.random.randint(len(far))]
    return np.exp2(a.ravel()).repeat(32)


BF16 = ml_dtypes.bfloat16


def bf(x):
    return np.asarray(x, np.float32).astype(BF16)


def f64(x):
    return np.asarray(x).astype(np.float64)


E2M1 = np.array([0.0, 0.5, 1.0, 1.5, 2.0, 3.0, 4.0, 6.0, -0.0, -0.5, -1.0, -1.5, -2.0, -3.0, -4.0, -6.0])


def pack_weight(w, fmt):
    k, n = w.shape
    w = f64(bf(w)).reshape(k // 32, 32, n)
    amax = np.abs(w).max(1)
    if fmt in ("e4m3", "e5m2"):
        byte = np.frexp(amax)[1] - 1 + 127 - (7 if fmt == "e4m3" else 14)
    else:
        mant, ex = np.frexp(amax / 6.0)
        byte = np.where(mant > 0.5, ex, ex - 1) + 127
    byte = np.clip(np.where(amax > 0, byte, 1), 1, 254)
    scaled = (w * np.exp2(127.0 - byte)[:, None, :]).reshape(k, n).astype(np.float32)
    by_word = np.ascontiguousarray(scaled.reshape(k // 512, 128, 4, n).transpose(0, 1, 3, 2))
    if fmt in ("e4m3", "e5m2"):
        words = by_word.astype(ml_dtypes.float8_e4m3fn if fmt == "e4m3" else ml_dtypes.float8_e5m2).view(np.uint8)
    else:
        c = by_word.astype(ml_dtypes.float4_e2m1fn).view(np.uint8) & 0xF
        words = c[..., 0::2] | (c[..., 1::2] << 4)
    return np.ascontiguousarray(words), np.ascontiguousarray(byte.astype(np.uint8).reshape(k // 512, 16, n))


def unpack_weight(words, scales, fmt):
    g, p, n, _ = words.shape
    if fmt in ("e4m3", "e5m2"):
        vals = np.ascontiguousarray(words).view(ml_dtypes.float8_e4m3fn if fmt == "e4m3" else ml_dtypes.float8_e5m2).astype(np.float64)
    else:
        nib = np.empty((g, p, n, 4), np.uint8)
        nib[..., 0::2] = words & 0xF
        nib[..., 1::2] = words >> 4
        vals = E2M1[nib]
    vals = vals * np.repeat(np.exp2(scales.astype(np.float64) - 127.0), 8, axis=1)[..., None]
    return vals.transpose(0, 1, 3, 2).reshape(g * 512, n)


P, A, T = 1024, 2048, 1536

STEP, PENALTY = 0.5, 0.3


def setup_inputs():
    s = mx_kscale(P)
    r = np.random.standard_t(4, (P, T)) * s[:, None]
    r_words, r_scales = pack_weight(r, "e5m2")
    d = np.random.standard_normal((P, A)) / np.sqrt(P) / s[:, None]
    z = np.maximum(np.random.standard_normal((A, T)), 0.0)
    step = STEP * (1.0 + 0.1 * np.random.standard_normal(A))
    lam = PENALTY + 0.2 * np.abs(np.random.standard_normal(A))
    return {"r_words": r_words,
            "r_scales": r_scales,
            "d": bf(d),
            "z": bf(z),
            "step": bf(step),
            "lam": bf(lam)}


def reference(r_words, r_scales, d, z, step, lam):
    r = unpack_weight(r_words, r_scales, "e5m2")
    dq = mxq(f64(d), 0, "e4m3")
    c = dq.T @ r
    moved = f64(z) + f64(step)[:, None] * (c - f64(lam)[:, None])
    return np.maximum(moved, 0.0)

@@ -1,0 +1,145 @@
+from contextlib import ExitStack
+
+import concourse.mybir as mybir
+from concourse.masks import make_identity
+
+F32 = mybir.dt.float32
+BF16 = mybir.dt.bfloat16
+I32 = mybir.dt.int32
+U32 = mybir.dt.uint32
+U8 = mybir.dt.uint8
+E4M3X4 = mybir.dt.float8_e4m3fn_x4
+E5M2X4 = mybir.dt.float8_e5m2_x4
+MULT = mybir.AluOpType.mult
+ADD = mybir.AluOpType.add
+RELU = mybir.ActivationFunctionType.Relu
+
+PIXELS, ATOMS, PATCHES = 1024, 2048, 1536
+FLOPS = 2 * PIXELS * ATOMS * PATCHES
+
+P = 128
+PACK = 4
+PASSES = PIXELS // (P * PACK)
+ROWS = 4
+BLOCK = P * ROWS
+BLOCKS = ATOMS // BLOCK
+BANK = 512
+LAM_ROW = 32
+
+
+def tile_nonnegative_sparse_coding_step_e1_kernel(tc, r_words, r_scales, d, z, step, lam, out):
+    nc = tc.nc
+    with ExitStack() as ctx:
+        keep = ctx.enter_context(tc.tile_pool(name="keep", bufs=1))
+        stage = ctx.enter_context(tc.tile_pool(name="stage", bufs=5))
+        results = ctx.enter_context(tc.tile_pool(name="results", bufs=8))
+        psum = ctx.enter_context(tc.psum_pool(name="psum", bufs=8))
+        ctx.enter_context(tc.manual_schedule())
+
+        d_view = d.rearrange("(g p j) a -> g p j a", p=P, j=PACK)
+        z_view = z.rearrange("(b m i) n -> b m i n", m=P, i=ROWS)
+        out_view = out.rearrange("(b m i) n -> b m i n", m=P, i=ROWS)
+        scale_view = r_scales.bitcast(I32).rearrange("g (q r) n -> r q g n", r=4)
+
+        r_sc = keep.tile([P, PASSES, PATCHES], U8, align_bytes=64, name="r_sc")
+        vec_rows = keep.tile([P, BLOCK], BF16, name="vec_rows")
+        ident = keep.tile([P, P], BF16, name="ident")
+        nc.vector.memset(vec_rows[:], 0.0)
+        nc.vector.memset(r_sc[:].bitcast(I32), 0)
+        make_identity(nc, ident[:])
+
+        raw = []
+        for g in range(PASSES):
+            t = keep.tile([P, PACK, ATOMS], BF16, align_bytes=64, name="raw%d" % g)
+            nc.sync.dma_start(out=t[:], in_=d_view[g])
+            raw.append(t)
+        nc.scalar.dma_start(out=vec_rows[0:BLOCKS, :], in_=step.rearrange("(b a) -> b a", b=BLOCKS))
+        nc.scalar.dma_start(out=vec_rows[LAM_ROW : LAM_ROW + BLOCKS, :], in_=lam.rearrange("(b a) -> b a", b=BLOCKS))
+        for r in range(4):
+            nc.scalar.dma_start(out=r_sc[r:P:32, :, :].bitcast(I32), in_=scale_view[r])
+        r_codes = []
+        for g in range(PASSES):
+            t = keep.tile([P, PATCHES], U32, align_bytes=64, name="r_codes%d" % g)
+            nc.sync.dma_start(out=t[:].bitcast(I32), in_=r_words[g].rearrange("p n t -> p (n t)").bitcast(I32))
+            r_codes.append(t)
+        z_sb = []
+        for b in range(BLOCKS):
+            t = keep.tile([P, ROWS, PATCHES], BF16, name="z_sb%d" % b)
+            cuts = [(0, 2), (2, 4)] if b == 0 else [(0, 4)]
+            for lo, hi in cuts:
+                nc.sync.dma_start(out=t[:, lo:hi, :], in_=z_view[b][:, lo:hi, :])
+            z_sb.append(t)
+
+        d_codes = {}
+        d_scales = {}
+        grouped = {}
+
+        def interleave(copy, g, b):
+            t = stage.tile([P, BLOCK * PACK], BF16, align_bytes=64, name="grouped")
+            copy(
+                out=t[:].rearrange("p (i m j) -> p i m j", i=ROWS, j=PACK),
+                in_=raw[g][:, :, b * BLOCK : (b + 1) * BLOCK].rearrange("p j (m i) -> p i m j", i=ROWS),
+            )
+            grouped[(g, b)] = t
+
+        def quantise(g, b):
+            codes = keep.tile([P, BLOCK], U32, align_bytes=64, name="d_codes%d%d" % (g, b))
+            scales = keep.tile([P, BLOCK], U8, align_bytes=64, name="d_scales%d%d" % (g, b))
+            nc.vector.quantize_mx(out=codes[:].bitcast(E4M3X4), scales=scales[:], in_=grouped[(g, b)][:])
+            d_codes[(g, b)] = codes
+            d_scales[(g, b)] = scales
+
+        vec = psum.tile([P, ROWS, P], BF16, name="bank")
+        rows_view = vec_rows[:].rearrange("p (m i) -> p i m", i=ROWS)
+        for i in range(ROWS):
+            nc.tensor.transpose(vec[:, i, :], rows_view[:, i, :], ident[:])
+
+        interleave(nc.vector.tensor_copy, 0, 0)
+        interleave(nc.scalar.copy, 0, 1)
+        interleave(nc.vector.tensor_copy, 0, 2)
+        interleave(nc.scalar.copy, 0, 3)
+        quantise(0, 0)
+        quantise(0, 2)
+        step_col = keep.tile([P, ROWS, BLOCKS], F32, name="step_col")
+        shift_col = keep.tile([P, ROWS, BLOCKS], F32, name="shift_col")
+        nc.vector.tensor_copy(out=step_col[:], in_=vec[:, :, 0:BLOCKS])
+        quantise(0, 1)
+        nc.vector.scalar_tensor_tensor(
+            out=shift_col[:], in0=vec[:, :, LAM_ROW : LAM_ROW + BLOCKS], scalar=-1.0, in1=step_col[:], op0=MULT, op1=MULT
+        )
+        interleave(nc.vector.tensor_copy, 1, 0)
+        interleave(nc.scalar.copy, 1, 1)
+        quantise(0, 3)
+        interleave(nc.vector.tensor_copy, 1, 2)
+        interleave(nc.scalar.copy, 1, 3)
+        quantise(1, 0)
+        quantise(1, 1)
+        quantise(1, 2)
+        quantise(1, 3)
+
+        for b in range(BLOCKS):
+            for h in range(2):
+                res = results.tile([P, 2, PATCHES], F32, name="res")
+                for e in range(2):
+                    i = 2 * h + e
+                    cols = slice(i * P, (i + 1) * P)
+                    for n0 in range(0, PATCHES, BANK):
+                        n = slice(n0, n0 + BANK)
+                        acc = psum.tile([P, BANK], F32, name="bank")
+                        for g in range(PASSES):
+                            nc.tensor.matmul_mx(
+                                out=acc[:],
+                                lhsT=d_codes[(g, b)][:, cols].bitcast(E4M3X4),
+                                lhsT_scale=d_scales[(g, b)][:, cols],
+                                rhs=r_codes[g][:, n].bitcast(E5M2X4),
+                                rhs_scale=r_sc[:, g, n],
+                                start=(g == 0),
+                                stop=(g == PASSES - 1),
+                            )
+                        nc.vector.scalar_tensor_tensor(
+                            out=res[:, e, n], in0=acc[:], scalar=step_col[:, i, b : b + 1], in1=z_sb[b][:, i, n], op0=MULT, op1=ADD
+                        )
+                    nc.scalar.activation(
+                        out=res[:, e, :], in_=res[:, e, :], func=RELU, bias=shift_col[:, i, b : b + 1], scale=1.0
+                    )
+                nc.sync.dma_start(out=out_view[b][:, 2 * h : 2 * h + 2, :], in_=res[:])

@@ -23,6 +23,9 @@ PASSES = PIXELS // (P * PACK)
 ROWS = 4
 BLOCK = P * ROWS
 BLOCKS = ATOMS // BLOCK
+HALVES = 2
+HALF = ATOMS // HALVES
+PER_HALF = BLOCKS // HALVES
 BANK = 512
 LAM_ROW = 32
 
@@ -36,7 +39,7 @@ def tile_nonnegative_sparse_coding_step_e1_kernel(tc, r_words, r_scales, d, z, s
         psum = ctx.enter_context(tc.psum_pool(name="psum", bufs=8))
         ctx.enter_context(tc.manual_schedule())
 
-        d_view = d.rearrange("(g p j) a -> g p j a", p=P, j=PACK)
+        d_view = d.rearrange("(g p j) (h a) -> h g p j a", p=P, j=PACK, h=HALVES)
         z_view = z.rearrange("(b m i) n -> b m i n", m=P, i=ROWS)
         out_view = out.rearrange("(b m i) n -> b m i n", m=P, i=ROWS)
         scale_view = r_scales.bitcast(I32).rearrange("g (q r) n -> r q g n", r=4)
@@ -48,27 +51,31 @@ def tile_nonnegative_sparse_coding_step_e1_kernel(tc, r_words, r_scales, d, z, s
         nc.vector.memset(r_sc[:].bitcast(I32), 0)
         make_identity(nc, ident[:])
 
-        raw = []
-        for g in range(PASSES):
-            t = keep.tile([P, PACK, ATOMS], BF16, align_bytes=64, name="raw%d" % g)
-            nc.sync.dma_start(out=t[:], in_=d_view[g])
-            raw.append(t)
-        nc.scalar.dma_start(out=vec_rows[0:BLOCKS, :], in_=step.rearrange("(b a) -> b a", b=BLOCKS))
-        nc.scalar.dma_start(out=vec_rows[LAM_ROW : LAM_ROW + BLOCKS, :], in_=lam.rearrange("(b a) -> b a", b=BLOCKS))
-        for r in range(4):
-            nc.scalar.dma_start(out=r_sc[r:P:32, :, :].bitcast(I32), in_=scale_view[r])
-        r_codes = []
-        for g in range(PASSES):
-            t = keep.tile([P, PATCHES], U32, align_bytes=64, name="r_codes%d" % g)
-            nc.sync.dma_start(out=t[:].bitcast(I32), in_=r_words[g].rearrange("p n t -> p (n t)").bitcast(I32))
-            r_codes.append(t)
+        raw = {}
+        for h in range(HALVES):
+            for g in range(PASSES):
+                raw[(h, g)] = keep.tile([P, PACK, HALF], BF16, align_bytes=64, name="raw%d%d" % (h, g))
+        r_codes = keep.tile([P, PASSES, PATCHES], U32, align_bytes=64, name="r_codes")
         z_sb = []
         for b in range(BLOCKS):
-            t = keep.tile([P, ROWS, PATCHES], BF16, name="z_sb%d" % b)
-            cuts = [(0, 2), (2, 4)] if b == 0 else [(0, 4)]
-            for lo, hi in cuts:
-                nc.sync.dma_start(out=t[:, lo:hi, :], in_=z_view[b][:, lo:hi, :])
-            z_sb.append(t)
+            z_sb.append(keep.tile([P, ROWS, PATCHES], BF16, name="z_sb%d" % b))
+
+        def load_z(b, lo, hi):
+            nc.sync.dma_start(out=z_sb[b][:, lo:hi, :], in_=z_view[b][:, lo:hi, :])
+
+        nc.scalar.dma_start(out=vec_rows[0:BLOCKS, :], in_=step.rearrange("(b a) -> b a", b=BLOCKS))
+        nc.scalar.dma_start(out=vec_rows[LAM_ROW : LAM_ROW + BLOCKS, :], in_=lam.rearrange("(b a) -> b a", b=BLOCKS))
+        for g in range(PASSES):
+            nc.sync.dma_start(out=raw[(0, g)][:], in_=d_view[0, g])
+        for r in range(4):
+            nc.sync.dma_start(out=r_sc[r:P:32, :, :].bitcast(I32), in_=scale_view[r])
+        nc.sync.dma_start(out=r_codes[:].bitcast(I32), in_=r_words.rearrange("g p n t -> p g (n t)").bitcast(I32))
+        load_z(0, 0, 2)
+        for g in range(PASSES):
+            nc.sync.dma_start(out=raw[(1, g)][:], in_=d_view[1, g])
+        load_z(0, 2, 4)
+        for b in range(1, BLOCKS):
+            load_z(b, 0, ROWS)
 
         d_codes = {}
         d_scales = {}
@@ -78,7 +85,9 @@ def tile_nonnegative_sparse_coding_step_e1_kernel(tc, r_words, r_scales, d, z, s
             t = stage.tile([P, BLOCK * PACK], BF16, align_bytes=64, name="grouped")
             copy(
                 out=t[:].rearrange("p (i m j) -> p i m j", i=ROWS, j=PACK),
-                in_=raw[g][:, :, b * BLOCK : (b + 1) * BLOCK].rearrange("p j (m i) -> p i m j", i=ROWS),
+                in_=raw[(b // PER_HALF, g)][:, :, b % PER_HALF * BLOCK : (b % PER_HALF + 1) * BLOCK].rearrange(
+                    "p j (m i) -> p i m j", i=ROWS
+                ),
             )
             grouped[(g, b)] = t
 
@@ -94,52 +103,53 @@ def tile_nonnegative_sparse_coding_step_e1_kernel(tc, r_words, r_scales, d, z, s
         for i in range(ROWS):
             nc.tensor.transpose(vec[:, i, :], rows_view[:, i, :], ident[:])
 
-        interleave(nc.vector.tensor_copy, 0, 0)
-        interleave(nc.scalar.copy, 0, 1)
-        interleave(nc.vector.tensor_copy, 0, 2)
-        interleave(nc.scalar.copy, 0, 3)
-        quantise(0, 0)
-        quantise(0, 2)
         step_col = keep.tile([P, ROWS, BLOCKS], F32, name="step_col")
         shift_col = keep.tile([P, ROWS, BLOCKS], F32, name="shift_col")
+
+        def tile_step(b, i, res):
+            cols = slice(i * P, (i + 1) * P)
+            for n0 in range(0, PATCHES, BANK):
+                n = slice(n0, n0 + BANK)
+                acc = psum.tile([P, BANK], F32, name="bank")
+                for g in range(PASSES):
+                    nc.tensor.matmul_mx(
+                        out=acc[:],
+                        lhsT=d_codes[(g, b)][:, cols].bitcast(E4M3X4),
+                        lhsT_scale=d_scales[(g, b)][:, cols],
+                        rhs=r_codes[:, g, n].bitcast(E5M2X4),
+                        rhs_scale=r_sc[:, g, n],
+                        start=(g == 0),
+                        stop=(g == PASSES - 1),
+                    )
+                nc.vector.scalar_tensor_tensor(
+                    out=res[:, i % 2, n], in0=acc[:], scalar=step_col[:, i, b : b + 1], in1=z_sb[b][:, i, n], op0=MULT, op1=ADD
+                )
+            nc.scalar.activation(
+                out=res[:, i % 2, :], in_=res[:, i % 2, :], func=RELU, bias=shift_col[:, i, b : b + 1], scale=1.0
+            )
+
+        interleave(nc.vector.tensor_copy, 0, 0)
         nc.vector.tensor_copy(out=step_col[:], in_=vec[:, :, 0:BLOCKS])
-        quantise(0, 1)
+        interleave(nc.scalar.copy, 1, 0)
+        quantise(0, 0)
         nc.vector.scalar_tensor_tensor(
             out=shift_col[:], in0=vec[:, :, LAM_ROW : LAM_ROW + BLOCKS], scalar=-1.0, in1=step_col[:], op0=MULT, op1=MULT
         )
-        interleave(nc.vector.tensor_copy, 1, 0)
+        interleave(nc.vector.tensor_copy, 0, 1)
         interleave(nc.scalar.copy, 1, 1)
-        quantise(0, 3)
-        interleave(nc.vector.tensor_copy, 1, 2)
-        interleave(nc.scalar.copy, 1, 3)
         quantise(1, 0)
+        quantise(0, 1)
         quantise(1, 1)
-        quantise(1, 2)
-        quantise(1, 3)
 
         for b in range(BLOCKS):
             for h in range(2):
                 res = results.tile([P, 2, PATCHES], F32, name="res")
-                for e in range(2):
-                    i = 2 * h + e
-                    cols = slice(i * P, (i + 1) * P)
-                    for n0 in range(0, PATCHES, BANK):
-                        n = slice(n0, n0 + BANK)
-                        acc = psum.tile([P, BANK], F32, name="bank")
-                        for g in range(PASSES):
-                            nc.tensor.matmul_mx(
-                                out=acc[:],
-                                lhsT=d_codes[(g, b)][:, cols].bitcast(E4M3X4),
-                                lhsT_scale=d_scales[(g, b)][:, cols],
-                                rhs=r_codes[g][:, n].bitcast(E5M2X4),
-                                rhs_scale=r_sc[:, g, n],
-                                start=(g == 0),
-                                stop=(g == PASSES - 1),
-                            )
-                        nc.vector.scalar_tensor_tensor(
-                            out=res[:, e, n], in0=acc[:], scalar=step_col[:, i, b : b + 1], in1=z_sb[b][:, i, n], op0=MULT, op1=ADD
-                        )
-                    nc.scalar.activation(
-                        out=res[:, e, :], in_=res[:, e, :], func=RELU, bias=shift_col[:, i, b : b + 1], scale=1.0
-                    )
+                for i in (2 * h, 2 * h + 1):
+                    tile_step(b, i, res)
                 nc.sync.dma_start(out=out_view[b][:, 2 * h : 2 * h + 2, :], in_=res[:])
+                if b < PER_HALF and h == 0:
+                    interleave(nc.vector.tensor_copy, 0, b + PER_HALF)
+                    interleave(nc.scalar.copy, 1, b + PER_HALF)
+                if b < PER_HALF and h == 1:
+                    quantise(0, b + PER_HALF)
+                    quantise(1, b + PER_HALF)

@@ -20,12 +20,15 @@ FLOPS = 2 * PIXELS * ATOMS * PATCHES
 P = 128
 PACK = 4
 PASSES = PIXELS // (P * PACK)
-ROWS = 4
-BLOCK = P * ROWS
-BLOCKS = ATOMS // BLOCK
+ROWS = 2
+PAIR = P * ROWS
+PAIRS = ATOMS // PAIR
+CHUNK = 512
+CHUNKS = ATOMS // CHUNK
+PAIRS_IN_CHUNK = CHUNK // PAIR
 HALVES = 2
 HALF = ATOMS // HALVES
-PER_HALF = BLOCKS // HALVES
+CHUNKS_IN_HALF = CHUNKS // HALVES
 BANK = 512
 LAM_ROW = 32
 
@@ -34,18 +37,18 @@ def tile_nonnegative_sparse_coding_step_e1_kernel(tc, r_words, r_scales, d, z, s
     nc = tc.nc
     with ExitStack() as ctx:
         keep = ctx.enter_context(tc.tile_pool(name="keep", bufs=1))
-        stage = ctx.enter_context(tc.tile_pool(name="stage", bufs=5))
+        stage = ctx.enter_context(tc.tile_pool(name="stage", bufs=4))
         results = ctx.enter_context(tc.tile_pool(name="results", bufs=8))
         psum = ctx.enter_context(tc.psum_pool(name="psum", bufs=8))
         ctx.enter_context(tc.manual_schedule())
 
         d_view = d.rearrange("(g p j) (h a) -> h g p j a", p=P, j=PACK, h=HALVES)
-        z_view = z.rearrange("(b m i) n -> b m i n", m=P, i=ROWS)
+        z_view = z.rearrange("(b m i) n -> m b (i n)", m=P, i=ROWS)
         out_view = out.rearrange("(b m i) n -> b m i n", m=P, i=ROWS)
         scale_view = r_scales.bitcast(I32).rearrange("g (q r) n -> r q g n", r=4)
 
         r_sc = keep.tile([P, PASSES, PATCHES], U8, align_bytes=64, name="r_sc")
-        vec_rows = keep.tile([P, BLOCK], BF16, name="vec_rows")
+        vec_rows = keep.tile([P, PAIR], BF16, name="vec_rows")
         ident = keep.tile([P, P], BF16, name="ident")
         nc.vector.memset(vec_rows[:], 0.0)
         nc.vector.memset(r_sc[:].bitcast(I32), 0)
@@ -56,84 +59,84 @@ def tile_nonnegative_sparse_coding_step_e1_kernel(tc, r_words, r_scales, d, z, s
             for g in range(PASSES):
                 raw[(h, g)] = keep.tile([P, PACK, HALF], BF16, align_bytes=64, name="raw%d%d" % (h, g))
         r_codes = keep.tile([P, PASSES, PATCHES], U32, align_bytes=64, name="r_codes")
-        z_sb = []
-        for b in range(BLOCKS):
-            z_sb.append(keep.tile([P, ROWS, PATCHES], BF16, name="z_sb%d" % b))
+        z_sb = keep.tile([P, PAIRS, ROWS * PATCHES], BF16, name="z_sb")
 
-        def load_z(b, lo, hi):
-            nc.sync.dma_start(out=z_sb[b][:, lo:hi, :], in_=z_view[b][:, lo:hi, :])
+        def load_z(lo, hi):
+            nc.sync.dma_start(out=z_sb[:, lo:hi, :], in_=z_view[:, lo:hi, :])
 
-        nc.scalar.dma_start(out=vec_rows[0:BLOCKS, :], in_=step.rearrange("(b a) -> b a", b=BLOCKS))
-        nc.scalar.dma_start(out=vec_rows[LAM_ROW : LAM_ROW + BLOCKS, :], in_=lam.rearrange("(b a) -> b a", b=BLOCKS))
+        nc.scalar.dma_start(out=vec_rows[0:PAIRS, :], in_=step.rearrange("(b a) -> b a", b=PAIRS))
+        nc.scalar.dma_start(out=vec_rows[LAM_ROW : LAM_ROW + PAIRS, :], in_=lam.rearrange("(b a) -> b a", b=PAIRS))
         for g in range(PASSES):
             nc.sync.dma_start(out=raw[(0, g)][:], in_=d_view[0, g])
         for r in range(4):
             nc.sync.dma_start(out=r_sc[r:P:32, :, :].bitcast(I32), in_=scale_view[r])
         nc.sync.dma_start(out=r_codes[:].bitcast(I32), in_=r_words.rearrange("g p n t -> p g (n t)").bitcast(I32))
-        load_z(0, 0, 2)
+        load_z(0, 1)
         for g in range(PASSES):
             nc.sync.dma_start(out=raw[(1, g)][:], in_=d_view[1, g])
-        load_z(0, 2, 4)
-        for b in range(1, BLOCKS):
-            load_z(b, 0, ROWS)
+        load_z(1, 2)
+        for b in range(2, PAIRS, 2):
+            load_z(b, b + 2)
 
         d_codes = {}
         d_scales = {}
         grouped = {}
 
-        def interleave(copy, g, b):
-            t = stage.tile([P, BLOCK * PACK], BF16, align_bytes=64, name="grouped")
-            copy(
-                out=t[:].rearrange("p (i m j) -> p i m j", i=ROWS, j=PACK),
-                in_=raw[(b // PER_HALF, g)][:, :, b % PER_HALF * BLOCK : (b % PER_HALF + 1) * BLOCK].rearrange(
-                    "p j (m i) -> p i m j", i=ROWS
-                ),
-            )
-            grouped[(g, b)] = t
+        def interleave(copy, g, c):
+            t = stage.tile([P, CHUNK * PACK], BF16, align_bytes=64, name="grouped")
+            for k in range(PAIRS_IN_CHUNK):
+                a = (c % CHUNKS_IN_HALF) * CHUNK + k * PAIR
+                copy(
+                    out=t[:, k * PAIR * PACK : (k + 1) * PAIR * PACK].rearrange("p (i m j) -> p i m j", i=ROWS, j=PACK),
+                    in_=raw[(c // CHUNKS_IN_HALF, g)][:, :, a : a + PAIR].rearrange("p j (m i) -> p i m j", i=ROWS),
+                )
+            grouped[(g, c)] = t
 
-        def quantise(g, b):
-            codes = keep.tile([P, BLOCK], U32, align_bytes=64, name="d_codes%d%d" % (g, b))
-            scales = keep.tile([P, BLOCK], U8, align_bytes=64, name="d_scales%d%d" % (g, b))
-            nc.vector.quantize_mx(out=codes[:].bitcast(E4M3X4), scales=scales[:], in_=grouped[(g, b)][:])
-            d_codes[(g, b)] = codes
-            d_scales[(g, b)] = scales
+        def quantise(g, c):
+            codes = keep.tile([P, CHUNK], U32, align_bytes=64, name="d_codes%d%d" % (g, c))
+            scales = keep.tile([P, CHUNK], U8, align_bytes=64, name="d_scales%d%d" % (g, c))
+            nc.vector.quantize_mx(out=codes[:].bitcast(E4M3X4), scales=scales[:], in_=grouped[(g, c)][:])
+            d_codes[(g, c)] = codes
+            d_scales[(g, c)] = scales
 
         vec = psum.tile([P, ROWS, P], BF16, name="bank")
         rows_view = vec_rows[:].rearrange("p (m i) -> p i m", i=ROWS)
         for i in range(ROWS):
             nc.tensor.transpose(vec[:, i, :], rows_view[:, i, :], ident[:])
-
-        step_col = keep.tile([P, ROWS, BLOCKS], F32, name="step_col")
-        shift_col = keep.tile([P, ROWS, BLOCKS], F32, name="shift_col")
+        step_col = keep.tile([P, ROWS, PAIRS], F32, name="step_col")
+        shift_col = keep.tile([P, ROWS, PAIRS], F32, name="shift_col")
 
         def tile_step(b, i, res):
-            cols = slice(i * P, (i + 1) * P)
+            c = b // PAIRS_IN_CHUNK
+            first = (b % PAIRS_IN_CHUNK) * PAIR + i * P
+            cols = slice(first, first + P)
             for n0 in range(0, PATCHES, BANK):
                 n = slice(n0, n0 + BANK)
+                zn = slice(i * PATCHES + n0, i * PATCHES + n0 + BANK)
                 acc = psum.tile([P, BANK], F32, name="bank")
                 for g in range(PASSES):
                     nc.tensor.matmul_mx(
                         out=acc[:],
-                        lhsT=d_codes[(g, b)][:, cols].bitcast(E4M3X4),
-                        lhsT_scale=d_scales[(g, b)][:, cols],
+                        lhsT=d_codes[(g, c)][:, cols].bitcast(E4M3X4),
+                        lhsT_scale=d_scales[(g, c)][:, cols],
                         rhs=r_codes[:, g, n].bitcast(E5M2X4),
                         rhs_scale=r_sc[:, g, n],
                         start=(g == 0),
                         stop=(g == PASSES - 1),
                     )
                 nc.vector.scalar_tensor_tensor(
-                    out=res[:, i % 2, n], in0=acc[:], scalar=step_col[:, i, b : b + 1], in1=z_sb[b][:, i, n], op0=MULT, op1=ADD
+                    out=res[:, i, n], in0=acc[:], scalar=step_col[:, i, b : b + 1], in1=z_sb[:, b, zn], op0=MULT, op1=ADD
                 )
             nc.scalar.activation(
-                out=res[:, i % 2, :], in_=res[:, i % 2, :], func=RELU, bias=shift_col[:, i, b : b + 1], scale=1.0
+                out=res[:, i, :], in_=res[:, i, :], func=RELU, bias=shift_col[:, i, b : b + 1], scale=1.0
             )
 
         interleave(nc.vector.tensor_copy, 0, 0)
-        nc.vector.tensor_copy(out=step_col[:], in_=vec[:, :, 0:BLOCKS])
+        nc.vector.tensor_copy(out=step_col[:], in_=vec[:, :, 0:PAIRS])
         interleave(nc.scalar.copy, 1, 0)
         quantise(0, 0)
         nc.vector.scalar_tensor_tensor(
-            out=shift_col[:], in0=vec[:, :, LAM_ROW : LAM_ROW + BLOCKS], scalar=-1.0, in1=step_col[:], op0=MULT, op1=MULT
+            out=shift_col[:], in0=vec[:, :, LAM_ROW : LAM_ROW + PAIRS], scalar=-1.0, in1=step_col[:], op0=MULT, op1=MULT
         )
         interleave(nc.vector.tensor_copy, 0, 1)
         interleave(nc.scalar.copy, 1, 1)
@@ -141,15 +144,15 @@ def tile_nonnegative_sparse_coding_step_e1_kernel(tc, r_words, r_scales, d, z, s
         quantise(0, 1)
         quantise(1, 1)
 
-        for b in range(BLOCKS):
-            for h in range(2):
-                res = results.tile([P, 2, PATCHES], F32, name="res")
-                for i in (2 * h, 2 * h + 1):
-                    tile_step(b, i, res)
-                nc.sync.dma_start(out=out_view[b][:, 2 * h : 2 * h + 2, :], in_=res[:])
-                if b < PER_HALF and h == 0:
-                    interleave(nc.vector.tensor_copy, 0, b + PER_HALF)
-                    interleave(nc.scalar.copy, 1, b + PER_HALF)
-                if b < PER_HALF and h == 1:
-                    quantise(0, b + PER_HALF)
-                    quantise(1, b + PER_HALF)
+        for b in range(PAIRS):
+            res = results.tile([P, ROWS, PATCHES], F32, name="res")
+            for i in range(ROWS):
+                tile_step(b, i, res)
+            nc.sync.dma_start(out=out_view[b], in_=res[:])
+            c = b // 2 + CHUNKS_IN_HALF
+            if c < CHUNKS and b % 2 == 0:
+                interleave(nc.vector.tensor_copy, 0, c)
+                interleave(nc.scalar.copy, 1, c)
+            if c < CHUNKS and b % 2 == 1:
+                quantise(0, c)
+                quantise(1, c)

@@ -26,9 +26,6 @@ PAIRS = ATOMS // PAIR
 CHUNK = 512
 CHUNKS = ATOMS // CHUNK
 PAIRS_IN_CHUNK = CHUNK // PAIR
-HALVES = 2
-HALF = ATOMS // HALVES
-CHUNKS_IN_HALF = CHUNKS // HALVES
 BANK = 512
 LAM_ROW = 32
 
@@ -37,12 +34,12 @@ def tile_nonnegative_sparse_coding_step_e1_kernel(tc, r_words, r_scales, d, z, s
     nc = tc.nc
     with ExitStack() as ctx:
         keep = ctx.enter_context(tc.tile_pool(name="keep", bufs=1))
-        stage = ctx.enter_context(tc.tile_pool(name="stage", bufs=4))
+        stage = ctx.enter_context(tc.tile_pool(name="stage", bufs=5))
         results = ctx.enter_context(tc.tile_pool(name="results", bufs=8))
         psum = ctx.enter_context(tc.psum_pool(name="psum", bufs=8))
         ctx.enter_context(tc.manual_schedule())
 
-        d_view = d.rearrange("(g p j) (h a) -> h g p j a", p=P, j=PACK, h=HALVES)
+        d_view = d.rearrange("(g p j) a -> g p j a", p=P, j=PACK)
         z_view = z.rearrange("(b m i) n -> m b (i n)", m=P, i=ROWS)
         out_view = out.rearrange("(b m i) n -> b m i n", m=P, i=ROWS)
         scale_view = r_scales.bitcast(I32).rearrange("g (q r) n -> r q g n", r=4)
@@ -54,10 +51,9 @@ def tile_nonnegative_sparse_coding_step_e1_kernel(tc, r_words, r_scales, d, z, s
         nc.vector.memset(r_sc[:].bitcast(I32), 0)
         make_identity(nc, ident[:])
 
-        raw = {}
-        for h in range(HALVES):
-            for g in range(PASSES):
-                raw[(h, g)] = keep.tile([P, PACK, HALF], BF16, align_bytes=64, name="raw%d%d" % (h, g))
+        raw = []
+        for g in range(PASSES):
+            raw.append(keep.tile([P, PACK, ATOMS], BF16, align_bytes=64, name="raw%d" % g))
         r_codes = keep.tile([P, PASSES, PATCHES], U32, align_bytes=64, name="r_codes")
         z_sb = keep.tile([P, PAIRS, ROWS * PATCHES], BF16, name="z_sb")
 
@@ -67,13 +63,11 @@ def tile_nonnegative_sparse_coding_step_e1_kernel(tc, r_words, r_scales, d, z, s
         nc.scalar.dma_start(out=vec_rows[0:PAIRS, :], in_=step.rearrange("(b a) -> b a", b=PAIRS))
         nc.scalar.dma_start(out=vec_rows[LAM_ROW : LAM_ROW + PAIRS, :], in_=lam.rearrange("(b a) -> b a", b=PAIRS))
         for g in range(PASSES):
-            nc.sync.dma_start(out=raw[(0, g)][:], in_=d_view[0, g])
+            nc.sync.dma_start(out=raw[g][:], in_=d_view[g])
         for r in range(4):
             nc.sync.dma_start(out=r_sc[r:P:32, :, :].bitcast(I32), in_=scale_view[r])
         nc.sync.dma_start(out=r_codes[:].bitcast(I32), in_=r_words.rearrange("g p n t -> p g (n t)").bitcast(I32))
         load_z(0, 1)
-        for g in range(PASSES):
-            nc.sync.dma_start(out=raw[(1, g)][:], in_=d_view[1, g])
         load_z(1, 2)
         for b in range(2, PAIRS, 2):
             load_z(b, b + 2)
@@ -85,10 +79,10 @@ def tile_nonnegative_sparse_coding_step_e1_kernel(tc, r_words, r_scales, d, z, s
         def interleave(copy, g, c):
             t = stage.tile([P, CHUNK * PACK], BF16, align_bytes=64, name="grouped")
             for k in range(PAIRS_IN_CHUNK):
-                a = (c % CHUNKS_IN_HALF) * CHUNK + k * PAIR
+                a = c * CHUNK + k * PAIR
                 copy(
                     out=t[:, k * PAIR * PACK : (k + 1) * PAIR * PACK].rearrange("p (i m j) -> p i m j", i=ROWS, j=PACK),
-                    in_=raw[(c // CHUNKS_IN_HALF, g)][:, :, a : a + PAIR].rearrange("p j (m i) -> p i m j", i=ROWS),
+                    in_=raw[g][:, :, a : a + PAIR].rearrange("p j (m i) -> p i m j", i=ROWS),
                 )
             grouped[(g, c)] = t
 
@@ -132,16 +126,23 @@ def tile_nonnegative_sparse_coding_step_e1_kernel(tc, r_words, r_scales, d, z, s
             )
 
         interleave(nc.vector.tensor_copy, 0, 0)
-        nc.vector.tensor_copy(out=step_col[:], in_=vec[:, :, 0:PAIRS])
-        interleave(nc.scalar.copy, 1, 0)
+        interleave(nc.scalar.copy, 0, 1)
+        interleave(nc.vector.tensor_copy, 0, 2)
+        interleave(nc.scalar.copy, 0, 3)
         quantise(0, 0)
+        nc.vector.tensor_copy(out=step_col[:], in_=vec[:, :, 0:PAIRS])
+        quantise(0, 1)
         nc.vector.scalar_tensor_tensor(
             out=shift_col[:], in0=vec[:, :, LAM_ROW : LAM_ROW + PAIRS], scalar=-1.0, in1=step_col[:], op0=MULT, op1=MULT
         )
-        interleave(nc.vector.tensor_copy, 0, 1)
+        interleave(nc.vector.tensor_copy, 1, 0)
         interleave(nc.scalar.copy, 1, 1)
+        quantise(0, 2)
         quantise(1, 0)
-        quantise(0, 1)
+        interleave(nc.vector.tensor_copy, 1, 2)
+        interleave(nc.scalar.copy, 1, 3)
+        quantise(0, 3)
+        quantise(1, 2)
         quantise(1, 1)
 
         for b in range(PAIRS):
@@ -149,10 +150,5 @@ def tile_nonnegative_sparse_coding_step_e1_kernel(tc, r_words, r_scales, d, z, s
             for i in range(ROWS):
                 tile_step(b, i, res)
             nc.sync.dma_start(out=out_view[b], in_=res[:])
-            c = b // 2 + CHUNKS_IN_HALF
-            if c < CHUNKS and b % 2 == 0:
-                interleave(nc.vector.tensor_copy, 0, c)
-                interleave(nc.scalar.copy, 1, c)
-            if c < CHUNKS and b % 2 == 1:
-                quantise(0, c)
-                quantise(1, c)
+            if b == 0:
+                quantise(1, 3)

from contextlib import ExitStack

import concourse.mybir as mybir
from concourse.masks import make_identity

F32 = mybir.dt.float32
BF16 = mybir.dt.bfloat16
I32 = mybir.dt.int32
U32 = mybir.dt.uint32
U8 = mybir.dt.uint8
E4M3X4 = mybir.dt.float8_e4m3fn_x4
E5M2X4 = mybir.dt.float8_e5m2_x4
MULT = mybir.AluOpType.mult
ADD = mybir.AluOpType.add
RELU = mybir.ActivationFunctionType.Relu

PIXELS, ATOMS, PATCHES = 1024, 2048, 1536
FLOPS = 2 * PIXELS * ATOMS * PATCHES

P = 128
PACK = 4
PASSES = PIXELS // (P * PACK)
ROWS = 2
PAIR = P * ROWS
PAIRS = ATOMS // PAIR
CHUNK = 512
CHUNKS = ATOMS // CHUNK
PAIRS_IN_CHUNK = CHUNK // PAIR
BANK = 512
LAM_ROW = 32


def tile_nonnegative_sparse_coding_step_e1_kernel(tc, r_words, r_scales, d, z, step, lam, out):
    nc = tc.nc
    with ExitStack() as ctx:
        keep = ctx.enter_context(tc.tile_pool(name="keep", bufs=1))
        stage = ctx.enter_context(tc.tile_pool(name="stage", bufs=5))
        results = ctx.enter_context(tc.tile_pool(name="results", bufs=8))
        psum = ctx.enter_context(tc.psum_pool(name="psum", bufs=8))
        ctx.enter_context(tc.manual_schedule())

        d_view = d.rearrange("(g p j) a -> g p j a", p=P, j=PACK)
        z_view = z.rearrange("(b m i) n -> m b (i n)", m=P, i=ROWS)
        out_view = out.rearrange("(b m i) n -> b m i n", m=P, i=ROWS)
        scale_view = r_scales.bitcast(I32).rearrange("g (q r) n -> r q g n", r=4)

        r_sc = keep.tile([P, PASSES, PATCHES], U8, align_bytes=64, name="r_sc")
        vec_rows = keep.tile([P, PAIR], BF16, name="vec_rows")
        ident = keep.tile([P, P], BF16, name="ident")
        nc.vector.memset(vec_rows[:], 0.0)
        nc.vector.memset(r_sc[:].bitcast(I32), 0)
        make_identity(nc, ident[:])

        raw = []
        for g in range(PASSES):
            raw.append(keep.tile([P, PACK, ATOMS], BF16, align_bytes=64, name="raw%d" % g))
        r_codes = keep.tile([P, PASSES, PATCHES], U32, align_bytes=64, name="r_codes")
        z_sb = keep.tile([P, PAIRS, ROWS * PATCHES], BF16, name="z_sb")

        def load_z(lo, hi):
            nc.sync.dma_start(out=z_sb[:, lo:hi, :], in_=z_view[:, lo:hi, :])

        nc.scalar.dma_start(out=vec_rows[0:PAIRS, :], in_=step.rearrange("(b a) -> b a", b=PAIRS))
        nc.scalar.dma_start(out=vec_rows[LAM_ROW : LAM_ROW + PAIRS, :], in_=lam.rearrange("(b a) -> b a", b=PAIRS))
        for g in range(PASSES):
            nc.sync.dma_start(out=raw[g][:], in_=d_view[g])
        for r in range(4):
            nc.sync.dma_start(out=r_sc[r:P:32, :, :].bitcast(I32), in_=scale_view[r])
        nc.sync.dma_start(out=r_codes[:].bitcast(I32), in_=r_words.rearrange("g p n t -> p g (n t)").bitcast(I32))
        load_z(0, 1)
        load_z(1, 2)
        for b in range(2, PAIRS, 2):
            load_z(b, b + 2)

        d_codes = {}
        d_scales = {}
        grouped = {}

        def interleave(copy, g, c):
            t = stage.tile([P, CHUNK * PACK], BF16, align_bytes=64, name="grouped")
            for k in range(PAIRS_IN_CHUNK):
                a = c * CHUNK + k * PAIR
                copy(
                    out=t[:, k * PAIR * PACK : (k + 1) * PAIR * PACK].rearrange("p (i m j) -> p i m j", i=ROWS, j=PACK),
                    in_=raw[g][:, :, a : a + PAIR].rearrange("p j (m i) -> p i m j", i=ROWS),
                )
            grouped[(g, c)] = t

        def quantise(g, c):
            codes = keep.tile([P, CHUNK], U32, align_bytes=64, name="d_codes%d%d" % (g, c))
            scales = keep.tile([P, CHUNK], U8, align_bytes=64, name="d_scales%d%d" % (g, c))
            nc.vector.quantize_mx(out=codes[:].bitcast(E4M3X4), scales=scales[:], in_=grouped[(g, c)][:])
            d_codes[(g, c)] = codes
            d_scales[(g, c)] = scales

        vec = psum.tile([P, ROWS, P], BF16, name="bank")
        rows_view = vec_rows[:].rearrange("p (m i) -> p i m", i=ROWS)
        for i in range(ROWS):
            nc.tensor.transpose(vec[:, i, :], rows_view[:, i, :], ident[:])
        step_col = keep.tile([P, ROWS, PAIRS], F32, name="step_col")
        shift_col = keep.tile([P, ROWS, PAIRS], F32, name="shift_col")

        def tile_step(b, i, res):
            c = b // PAIRS_IN_CHUNK
            first = (b % PAIRS_IN_CHUNK) * PAIR + i * P
            cols = slice(first, first + P)
            for n0 in range(0, PATCHES, BANK):
                n = slice(n0, n0 + BANK)
                zn = slice(i * PATCHES + n0, i * PATCHES + n0 + BANK)
                acc = psum.tile([P, BANK], F32, name="bank")
                for g in range(PASSES):
                    nc.tensor.matmul_mx(
                        out=acc[:],
                        lhsT=d_codes[(g, c)][:, cols].bitcast(E4M3X4),
                        lhsT_scale=d_scales[(g, c)][:, cols],
                        rhs=r_codes[:, g, n].bitcast(E5M2X4),
                        rhs_scale=r_sc[:, g, n],
                        start=(g == 0),
                        stop=(g == PASSES - 1),
                    )
                nc.vector.scalar_tensor_tensor(
                    out=res[:, i, n], in0=acc[:], scalar=step_col[:, i, b : b + 1], in1=z_sb[:, b, zn], op0=MULT, op1=ADD
                )
            nc.scalar.activation(
                out=res[:, i, :], in_=res[:, i, :], func=RELU, bias=shift_col[:, i, b : b + 1], scale=1.0
            )

        interleave(nc.vector.tensor_copy, 0, 0)
        interleave(nc.scalar.copy, 0, 1)
        interleave(nc.vector.tensor_copy, 0, 2)
        interleave(nc.scalar.copy, 0, 3)
        quantise(0, 0)
        nc.vector.tensor_copy(out=step_col[:], in_=vec[:, :, 0:PAIRS])
        quantise(0, 1)
        nc.vector.scalar_tensor_tensor(
            out=shift_col[:], in0=vec[:, :, LAM_ROW : LAM_ROW + PAIRS], scalar=-1.0, in1=step_col[:], op0=MULT, op1=MULT
        )
        interleave(nc.vector.tensor_copy, 1, 0)
        interleave(nc.scalar.copy, 1, 1)
        quantise(0, 2)
        quantise(1, 0)
        interleave(nc.vector.tensor_copy, 1, 2)
        interleave(nc.scalar.copy, 1, 3)
        quantise(0, 3)
        quantise(1, 2)
        quantise(1, 1)

        for b in range(PAIRS):
            res = results.tile([P, ROWS, PATCHES], F32, name="res")
            for i in range(ROWS):
                tile_step(b, i, res)
            nc.sync.dma_start(out=out_view[b], in_=res[:])
            if b == 0:
                quantise(1, 3)
